import numpy as np
CORES = [12,28,60,100,156,228]
N = 6
R, B, K = 256, 128, 4
T = B * K
def entries(a): return a.T.reshape(-1)
def pack(v, P): return np.ascontiguousarray(np.asarray(v, np.int32).reshape(-1, P).T)
def lists(rng, how):
    I = rng.integers(0, N * R, (N, T))
    if how == "alike": I[:] = rng.integers(0, N * R, (N, 1))
    if how == "distinct": I = np.stack([rng.permutation(N * R)[:T] for r in range(N)])
    if how == "hotrank": I = R * int(rng.integers(N)) + rng.integers(0, R, (N, T))
    if how == "own": I = R * np.arange(N).reshape(N, 1) + rng.integers(0, R, (N, T))
    if how == "edge": I = R * rng.integers(0, N, (N, T)) + np.where(rng.random((N, T)) < 0.5, 0, R - 1)
    return {"idx": np.stack([pack(I[r], 16) for r in range(N)])}
def setup_inputs(rng):
    return dict({"tab": rng.standard_normal((N, 128, R), dtype=np.float32)}, **lists(rng, "uniform"))
def setup_inputs_alike(rng):
    d = setup_inputs(rng); d.update(lists(rng, "alike"))
    for k in ("tab",): d[k] = (d[k].astype(np.float32) * 1024.0).astype(d[k].dtype)
    return d
def setup_inputs_distinct(rng):
    d = setup_inputs(rng); d.update(lists(rng, "distinct"))
    for k in ("tab",): d[k] = (d[k].astype(np.float32) * (1 / 1024.0)).astype(d[k].dtype)
    return d
def setup_inputs_edge(rng):
    d = setup_inputs(rng); d.update(lists(rng, "edge"))
    return d
def setup_inputs_hotrank(rng):
    d = setup_inputs(rng); d.update(lists(rng, "hotrank"))
    return d
def setup_inputs_own(rng):
    d = setup_inputs(rng); d.update(lists(rng, "own"))
    return d
def check_inputs(x):
    bad = []
    if x["idx"].min() < 0 or x["idx"].max() >= N * R: bad.append("idx out of range")
    return bad
def reference(tab, idx):
    A = np.concatenate(list(tab), axis=1).astype(np.float64)
    return {"y": np.stack([A[:, entries(idx[r])].reshape(128, B, K).sum(axis=2) for r in range(N)]).astype(np.float32)}

from concourse.bass import DstId, RemoteDMATransfer
from concourse.mybir import AluOpType, ActivationFunctionType

N, R, B, K = 6, 256, 128, 4
NSIM = 256
PIECES = 4
EP = B * K // PIECES

SCRATCH = {
    "win": ("sbuf", [128, N * R], "float32"),
    "ix": ("sbuf", [128, B * K // 16], "int32"),
    "off": ("sbuf", [128, B * K // 16], "uint16"),
    "gat": ("sbuf", [128, B * K], "float32"),
    "two": ("sbuf", [128, B * K // 2], "float32"),
    "yb": ("sbuf", [128, B], "float32"),
}
SEMAPHORES = ["ld", "li", "cv", "arr", "sent", "g0", "g1", "g2", "g3", "ad", "st"]


def _count(mask):
    return bin(mask).count("1")


def _plan(T, topo):
    cores = [int(c) for c in T.cores]
    calls, jobs = {}, {}
    for r, c in enumerate(cores):
        chip = [x for x in range(NSIM) if x not in cores
                and topo.host(x) == topo.host(c) and topo.chip(x) == topo.chip(c)]
        plane = [q for q in range(N) if q == r or topo.may_write(c, cores[q])]
        far = [q for q in range(N) if q not in plane]
        pos = plane.index(r)
        near = [plane[(pos + j) % len(plane)] for j in range(1, len(plane))]
        s = pos * len(far) // len(plane)
        far = far[s:] + far[:s]
        owners = [x for x in chip if all(topo.may_write(x, cores[q]) for q in far)]
        here = [x for x in owners if topo.die(x) == topo.die(c)]
        there = [x for x in owners if topo.die(x) != topo.die(c)]
        every = topo.mask(c, chip[0])
        out = topo.mask(c, cores[near[0]])
        stay = every & ~out
        if len(far) == 2:
            first = (here if pos % 2 == 0 else there)[0]
            third = [x for x in chip if topo.die(x) != topo.die(c) and x != first][0]
            calls[c] = [[(every, [first])],
                        [(out, [cores[q] for q in near[:2]]), (stay, [third])]]
            more = [(third, stay, near[2:])]
        else:
            first = there[0]
            calls[c] = [[(every, [first])],
                        [(out, [here[0]]), (stay, [here[1]])],
                        [(out, [cores[q] for q in near])]]
            more = [(here[0], out, far[2:3]), (here[1], stay, far[3:4])]
        for h, m, dst in [(first, every, far[:2])] + more:
            jobs[h] = (r, _count(m), topo.mask(h, cores[dst[0]]), [cores[q] for q in dst])
    return calls, jobs


def _send(g, core, T, topo, slot, call):
    if len(call) == 1 and len(call[0][1]) == 1:
        mask, (d,) = call[0]
        rid, pid = topo.addr(d, core)
        g.remote_dma(slot, slot, T.sem.arr, T.sem.sent, pid, rid, mask)
        return _count(mask)
    trs = []
    for mask, dst in call:
        ids = []
        for d in dst:
            rid, pid = topo.addr(d, core)
            ids.append(DstId(rid=rid, pnc=pid))
        trs.append(RemoteDMATransfer(dst_ids=ids, dma_engine_mask=mask, remote_sem=T.sem.arr,
                                     srcs=[slot], dsts=[slot for _ in dst], alu_op=0))
    g.remote_dma_fused(trs, local_sem=T.sem.sent)
    return sum(_count(mask) for mask, _ in call)


def rank_program(g, core, T, topo):
    calls, jobs = _plan(T, topo)
    rank = T.rank_of(core)

    if rank is None:
        if core not in jobs:
            return
        r, need, mask, dst = jobs[core]
        slot = T.win[:, r * R:(r + 1) * R]
        g.wait_ge(T.sem.arr, need)
        n = _send(g, core, T, topo, slot, [(mask, dst)])
        g.wait_ge(T.sem.sent, n)
        return

    slot = T.win[:, rank * R:(rank + 1) * R]
    g.sync.dma_start(slot, T.tab[:]).then_inc(T.sem.ld, 16)
    for k in range(8):
        g.scalar.dma_start(T.ix[16 * k:16 * k + 16, :], T.idx[:]).then_inc(T.sem.li, 16)

    g.wait_ge(T.sem.ld, 16)
    n = 0
    for call in calls[core]:
        n += _send(g, core, T, topo, slot, call)

    v, s = g.vector, g.scalar
    v.wait_ge(T.sem.li, 16 * 8)
    v.tensor_copy(T.off[:], T.ix[:]).then_inc(T.sem.cv, 1)

    landed = (N - 1) * _count(topo.mask(core, [int(c) for c in T.cores if int(c) != core
                                               and topo.may_write(core, int(c))][0]))
    oc = EP // 16
    for q in (v, s):
        q.wait_ge(T.sem.cv, 1)
        q.wait_ge(T.sem.ld, 16)
        q.wait_ge(T.sem.arr, landed)
    v.tensor_copy(T.gat[:, 0:EP], T.win[:, 0:N * R].indirect(T.off[:, 0:oc])).then_inc(T.sem.g0, 1)
    for i in range(1, PIECES):
        s.activation(T.gat[:, i * EP:(i + 1) * EP], T.win[:, 0:N * R].indirect(T.off[:, i * oc:(i + 1) * oc]),
                     ActivationFunctionType.Copy).then_inc(T.sem["g%d" % i], 1)
    for i in range(PIECES):
        a, h, y = i * EP, i * EP // 2, i * EP // 4
        v.wait_ge(T.sem["g%d" % i], 1)
        v.tensor_tensor(T.two[:, h:h + EP // 2], T.gat[:, a:a + EP:2], T.gat[:, a + 1:a + EP:2],
                        AluOpType.add).then_inc(T.sem.ad, 1)
        v.wait_ge(T.sem.ad, 2 * i + 1)
        v.tensor_tensor(T.yb[:, y:y + EP // 4], T.two[:, h:h + EP // 2:2], T.two[:, h + 1:h + EP // 2:2],
                        AluOpType.add).then_inc(T.sem.ad, 1)

    g.sync.wait_ge(T.sem.ad, 2 * PIECES)
    g.sync.dma_start(T.y[:], T.yb[:]).then_inc(T.sem.st, 16)
    g.sync.wait_ge(T.sem.st, 16)
    g.wait_ge(T.sem.sent, n)
